import numpy as np
import ml_dtypes


def mxq(x, axis, fmt="e4m3"):
    dtype, down = {"e4m3": (ml_dtypes.float8_e4m3fn, 7), "e5m2": (ml_dtypes.float8_e5m2, 14)}[fmt]
    v = np.moveaxis(np.asarray(x, np.float32).astype(ml_dtypes.bfloat16).astype(np.float64), axis, -1)
    blocks = v.reshape(v.shape[:-1] + (-1, 32))
    amax = np.abs(blocks).max(-1, keepdims=True)
    byte = np.maximum(np.where(amax > 0, np.frexp(amax)[1] - 1 + 127, 0) - down, 1)
    scale = np.exp2(byte - 127.0)
    codes = (blocks / scale).astype(np.float32).astype(dtype).astype(np.float64)
    return np.moveaxis((codes * scale).reshape(v.shape), -1, axis)


WIDE = False


def mx_kscale(k):
    if not WIDE:
        return np.ones(k)
    levels = np.array([10, -10, 5, -5, 0])
    if k % 512:
        return np.exp2(np.random.permutation(np.resize(levels, k // 32))).repeat(32)
    a = np.empty((k // 512, 16))
    for p in range(k // 512):
        a[p, :8] = np.random.permutation(np.resize(levels, 8))
        for g in range(8):
            far = levels[np.abs(levels - a[p, g]) >= 10]
            a[p, g + 8] = far[np.random.randint(len(far))]
    return np.exp2(a.ravel()).repeat(32)


BF16 = ml_dtypes.bfloat16


def bf(x):
    return np.asarray(x, np.float32).astype(BF16)


def f64(x):
    return np.asarray(x).astype(np.float64)


E2M1 = np.array([0.0, 0.5, 1.0, 1.5, 2.0, 3.0, 4.0, 6.0, -0.0, -0.5, -1.0, -1.5, -2.0, -3.0, -4.0, -6.0])


def pack_weight(w, fmt):
    k, n = w.shape
    w = f64(bf(w)).reshape(k // 32, 32, n)
    amax = np.abs(w).max(1)
    if fmt == "e4m3":
        byte = np.frexp(amax)[1] - 1 + 127 - 7
    else:
        mant, ex = np.frexp(amax / 6.0)
        byte = np.where(mant > 0.5, ex, ex - 1) + 127
    byte = np.clip(np.where(amax > 0, byte, 1), 1, 254)
    scaled = (w * np.exp2(127.0 - byte)[:, None, :]).reshape(k, n).astype(np.float32)
    by_word = np.ascontiguousarray(scaled.reshape(k // 512, 128, 4, n).transpose(0, 1, 3, 2))
    if fmt == "e4m3":
        words = by_word.astype(ml_dtypes.float8_e4m3fn).view(np.uint8)
    else:
        c = by_word.astype(ml_dtypes.float4_e2m1fn).view(np.uint8) & 0xF
        words = c[..., 0::2] | (c[..., 1::2] << 4)
    return np.ascontiguousarray(words), np.ascontiguousarray(byte.astype(np.uint8).reshape(k // 512, 16, n))


def unpack_weight(words, scales, fmt):
    g, p, n, _ = words.shape
    if fmt == "e4m3":
        vals = np.ascontiguousarray(words).view(ml_dtypes.float8_e4m3fn).astype(np.float64)
    else:
        nib = np.empty((g, p, n, 4), np.uint8)
        nib[..., 0::2] = words & 0xF
        nib[..., 1::2] = words >> 4
        vals = E2M1[nib]
    vals = vals * np.repeat(np.exp2(scales.astype(np.float64) - 127.0), 8, axis=1)[..., None]
    return vals.transpose(0, 1, 3, 2).reshape(g * 512, n)
def pack4(w):
    words, scales = pack_weight(w, "e2m1")
    return words.reshape(words.shape[0], 128, -1), scales


def unpack4(words, scales):
    return unpack_weight(words.reshape(words.shape[0], 128, -1, 2), scales, "e2m1")


def planes(Y):
    n, m = Y.shape
    b = f64(bf(Y)).reshape(n // 32, 32, m)
    amax = np.abs(b).max(1)
    byte = np.clip(np.where(amax > 0, np.frexp(amax)[1] - 1 + 127 - 7, 1), 1, 254)
    codes = (b * np.exp2(127.0 - byte)[:, None, :]).reshape(n, m).astype(np.float32).astype(ml_dtypes.float8_e4m3fn).view(np.uint8)
    words = codes.reshape(n // 512, 128, 4, m).transpose(0, 1, 3, 2)
    return np.ascontiguousarray(words), np.ascontiguousarray(byte.astype(np.uint8).reshape(n // 512, 16, m))


T, FS, FR, D = 768, 1024, 2048, 1536

def setup_inputs():
    rand, randn = np.random.rand, np.random.randn
    s = mx_kscale(FS)
    r = mx_kscale(FR)
    shared_h = bf(randn(T, FS) * s)
    shared_w = bf(randn(FS, D) / np.sqrt(FS) / s[:, None])
    routed_h = bf(randn(T, FR) * r)
    routed_w_words, routed_w_scales = pack4(randn(FR, D) / np.sqrt(FR) / r[:, None])
    gate = bf(0.3 + 0.6 * rand(T))
    x = bf(0.8 * randn(T, D))
    smooth = bf(np.exp(0.8 * randn(D)))
    return {"shared_h": shared_h, "shared_w": shared_w, "routed_h": routed_h,
            "routed_w_words": routed_w_words, "routed_w_scales": routed_w_scales,
            "gate": gate, "x": x, "smooth": smooth}

def reference(shared_h, shared_w, routed_h, routed_w_words, routed_w_scales, gate, x, smooth):
    hs = mxq(f64(shared_h), 1, "e4m3")
    ws = mxq(f64(shared_w), 0, "e4m3")
    shared = hs @ ws
    hr = mxq(f64(routed_h), 1, "e4m3")
    wr = unpack4(routed_w_words, routed_w_scales)
    routed = hr @ wr
    y = (shared + f64(gate)[:, None] * routed + f64(x)) * f64(smooth)[None, :]
    Y = y.T
    words, scales = planes(Y)
    return y, words, scales

@@ -1,0 +1,316 @@
+from contextlib import ExitStack
+
+import concourse.mybir as mybir
+from concourse.masks import make_identity
+
+T, FS, FR, D = 768, 1024, 2048, 1536
+FLOPS = 2 * T * (FS + FR) * D
+
+F32 = mybir.dt.float32
+BF16 = mybir.dt.bfloat16
+I32 = mybir.dt.int32
+U32 = mybir.dt.uint32
+U8 = mybir.dt.uint8
+FP8X4 = mybir.dt.float8_e4m3fn_x4
+FP4X4 = mybir.dt.float4_e2m1fn_x4
+ADD = mybir.AluOpType.add
+MULT = mybir.AluOpType.mult
+
+P = 128
+KP = 512
+NC = 512
+TILES = T // P
+CHUNKS = D // NC
+UNITS = TILES * CHUNKS
+SP_ = FS // KP
+RP_ = FR // KP
+
+LEAD = 2
+EARLY = 4
+LATE_AT = 3
+W1_AFTER = 2
+W_AT = (-3, 3, 7)
+W_ON_VECTOR = ((0, 0), (0, 1), (1, 0))
+HS_AHEAD = 1.4
+HR_AT = 1.1
+Y_RUN = 3
+Y_AGE = 3
+ROUND_DELAY = 1
+Q_DELAY = 1
+W_PARTS = 4
+W_RATE = (8, 2)
+
+
+def tile_shared_routed_expert_merge_g5_kernel(
+    tc, shared_h, shared_w, routed_h, routed_w_words, routed_w_scales, gate, x, smooth, out_0, out_1, out_2
+):
+    nc = tc.nc
+    with ExitStack() as ctx:
+        keep = ctx.enter_context(tc.tile_pool(name="keep", bufs=1))
+        work = ctx.enter_context(tc.tile_pool(name="work", bufs=2))
+        mm_psum = ctx.enter_context(tc.psum_pool(name="mm_psum", bufs=4))
+        tr_psum = ctx.enter_context(tc.psum_pool(name="tr_psum", bufs=4))
+        ctx.enter_context(tc.manual_schedule(engines={mybir.EngineType.PE, mybir.EngineType.SP}))
+
+        hr_raw, hs_raw, x_sb, ws_raw, wr_words = {}, {}, {}, {}, {}
+        hr_mx, hs_mx, ws_mx, partial, y_sorted, ws_grouped = {}, {}, {}, {}, {}, {}
+
+        def rows(i):
+            return slice(i * P, (i + 1) * P)
+
+        def cols(c):
+            return slice(c * NC, (c + 1) * NC)
+
+        def load_hr(i):
+            hr_raw[i] = keep.tile([P, FR], BF16, name="hr_raw%d" % i)
+            nc.sync.dma_start(out=hr_raw[i][:], in_=routed_h[rows(i), :])
+
+        def load_hs(i):
+            hs_raw[i] = keep.tile([P, FS], BF16, name="hs_raw%d" % i)
+            nc.sync.dma_start(out=hs_raw[i][:], in_=shared_h[rows(i), :])
+
+        def load_x(i, c0, c1):
+            t = keep.tile([P, (c1 - c0) * NC], BF16, name="x_sb%d%d" % (i, c0))
+            nc.sync.dma_start(out=t[:], in_=x[rows(i), c0 * NC : c1 * NC])
+            for c in range(c0, c1):
+                x_sb[i, c] = t[:, cols(c - c0)]
+
+        def load_wr(c):
+            wr_words[c] = keep.tile([P, RP_, 2 * NC], U8, name="wr_words%d" % c, align_bytes=64)
+            src = routed_w_words[:, :, 2 * NC * c : 2 * NC * (c + 1)].rearrange("g p b -> p g b")
+            nc.sync.dma_start(out=wr_words[c][:].bitcast(I32), in_=src.bitcast(I32))
+
+        def load_wr_scales(c):
+            for q in range(4):
+                nc.sync.dma_start(
+                    out=wr_scales[c][32 * q : 32 * q + 4, :, :].bitcast(I32),
+                    in_=routed_w_scales[:, 4 * q : 4 * q + 4, cols(c)].rearrange("g r n -> r g n").bitcast(I32),
+                )
+
+        def load_ws(c, g):
+            ws_raw[c, g] = keep.tile([P, 4, NC], BF16, name="ws_raw%d%d" % (c, g))
+            src = shared_w[g * KP : (g + 1) * KP, cols(c)].rearrange("(p j) n -> p j n", j=4)
+            nc.sync.dma_start(out=ws_raw[c, g][:], in_=src)
+
+        wr_scales = {}
+        for c in range(CHUNKS):
+            wr_scales[c] = keep.tile([P, RP_, NC], U8, name="wr_scales%d" % c, align_bytes=64)
+            nc.vector.memset(wr_scales[c][:].rearrange("p g n -> p (g n)").bitcast(I32), 0)
+        load_hr(0)
+        gate_rows = keep.tile([TILES, P], BF16, name="gate_rows")
+        smooth_words = keep.tile([P, CHUNKS, 4], BF16, name="smooth_words")
+        nc.scalar.dma_start(out=gate_rows[:], in_=gate.rearrange("(i p) -> i p", p=P))
+        nc.scalar.dma_start(out=smooth_words[:], in_=smooth.rearrange("(c p t) -> p c t", c=CHUNKS, t=4))
+        ident = keep.tile([P, P], F32, name="ident")
+        make_identity(nc, ident[:])
+        load_wr_scales(0)
+        load_wr(0)
+        load_hr(1)
+        load_ws(0, 0)
+        load_ws(0, 1)
+        for i in range(TILES):
+            load_x(i, 0, 1)
+            load_hs(i)
+            if i + 2 < TILES:
+                load_hr(i + 2)
+            if i == W1_AFTER:
+                load_ws(1, 0)
+            if i == W1_AFTER + 1:
+                load_ws(1, 1)
+        late = [lambda: load_wr_scales(1), lambda: load_wr(1)]
+        late = late + [lambda: load_x(0, 1, 3), lambda: load_ws(2, 0), lambda: load_x(1, 1, 3), lambda: load_ws(2, 1)]
+        late = late + [lambda i=i: load_x(i, 1, 3) for i in range(2, TILES)]
+        late = late + [lambda: load_wr_scales(2), lambda: load_wr(2)]
+        for n in range(EARLY):
+            late.pop(0)()
+
+        gate_pad = keep.tile([P, P], F32, name="gate_pad")
+        gate_col = keep.tile([P, TILES], F32, name="gate_col")
+        smooth_all = keep.tile([P, D], BF16, name="smooth_all")
+        y_words = keep.tile([P, CHUNKS, T], U32, name="y_words", align_bytes=64)
+        y_scales = keep.tile([P, CHUNKS, T], U8, name="y_scales", align_bytes=64)
+
+        def unzip_bank(dst_bf16, bank, pairs):
+            nc.scalar.copy(
+                out=dst_bf16.bitcast(F32).rearrange("p (g r u) -> p g r u", g=pairs, u=2),
+                in_=bank[:, : 2 * pairs, :].rearrange("p (g u) r -> p g r u", u=2),
+            )
+
+        def spread_vectors():
+            nc.vector.memset(gate_pad[:], 0.0)
+            nc.vector.tensor_copy(out=gate_pad[:TILES, :], in_=gate_rows[:])
+            words = smooth_words[:].rearrange("p c t -> p (c t)").bitcast(F32)
+            first = tr_psum.tile([P, 4, P], F32, name="tr_bank")
+            second = tr_psum.tile([P, 4, P], F32, name="tr_bank")
+            for w in range(2 * CHUNKS):
+                bank = first if w < 4 else second
+                nc.tensor.transpose(bank[:, w % 4, :], words[:, w : w + 1].to_broadcast([P, P]), ident[:])
+            nc.tensor.transpose(second[:, 2, :], gate_pad[:], ident[:])
+            nc.scalar.copy(out=gate_col[:], in_=second[:, 2, :TILES])
+            unzip_bank(smooth_all[:, : 2 * NC], first, 2)
+            unzip_bank(smooth_all[:, 2 * NC :], second, 1)
+
+        later = []
+        clock = [0]
+
+        def defer(steps_ahead, fn):
+            later.append((clock[0] + steps_ahead, fn))
+
+        def turn_h(raw, passes, tag, store, i):
+            words = raw[:].bitcast(F32)
+            turned = work.tile([P, passes * KP], BF16, name=tag + "_turned", align_bytes=64)
+            for g0 in range(0, passes, 2):
+                bank = tr_psum.tile([P, 4, P], F32, name="tr_bank")
+                for g in range(2):
+                    for u in range(2):
+                        first = 256 * (g0 + g) + u
+                        nc.tensor.transpose(bank[:, 2 * g + u, :], words[:, first : 256 * (g0 + g + 1) : 2], ident[:])
+                unzip_bank(turned[:, g0 * KP : (g0 + 2) * KP], bank, 2)
+            codes = work.tile([P, passes * P], U32, name=tag + "_codes", bufs=6, align_bytes=64)
+            scales = work.tile([P, passes * P], U8, name=tag + "_scales", bufs=6, align_bytes=64)
+            store[i] = (codes, scales)
+            return lambda: nc.vector.quantize_mx(out=codes[:].bitcast(FP8X4), scales=scales[:], in_=turned[:])
+
+        def group_ws(piece):
+            c, g, h = piece
+            if h == 0:
+                ws_grouped[c, g] = work.tile([P, NC, 4], BF16, name="ws_grouped", bufs=3, align_bytes=64)
+            grouped = ws_grouped[c, g]
+            part = slice(h * NC // W_PARTS, (h + 1) * NC // W_PARTS)
+            dst = grouped[:, part, :].rearrange("p (n i) t -> p n t i", i=4)
+            src = ws_raw[c, g][:, :, part].rearrange("p t (n i) -> p n t i", i=4)
+            if (c, g) in W_ON_VECTOR:
+                nc.vector.tensor_copy(out=dst, in_=src)
+            else:
+                nc.scalar.copy(out=dst, in_=src)
+            if h == W_PARTS - 1:
+                codes = keep.tile([P, NC], U32, name="ws_codes%d%d" % (c, g), align_bytes=64)
+                scales = keep.tile([P, NC], U8, name="ws_scales%d%d" % (c, g), align_bytes=64)
+                ws_mx[c, g] = (codes, scales)
+                defer(
+                    1,
+                    lambda: nc.vector.quantize_mx(
+                        out=codes[:].bitcast(FP8X4), scales=scales[:], in_=grouped[:].rearrange("p n t -> p (n t)")
+                    ),
+                )
+
+        def routed_pass(acc, i, c, g):
+            codes, scales = hr_mx[i]
+            nc.tensor.matmul_mx(
+                out=acc[:],
+                lhsT=codes[:, rows(g)].bitcast(FP8X4),
+                lhsT_scale=scales[:, rows(g)],
+                rhs=wr_words[c][:, g, :].bitcast(FP4X4),
+                rhs_scale=wr_scales[c][:, g, :],
+                start=(g == 0),
+                stop=(g == RP_ - 1),
+            )
+
+        def gate_and_residual(acc, i, c):
+            partial[i, c] = work.tile([P, NC], F32, name="partial", bufs=5)
+            nc.vector.scalar_tensor_tensor(
+                out=partial[i, c][:], in0=acc[:], scalar=gate_col[:, i : i + 1], in1=x_sb[i, c],
+                op0=MULT, op1=ADD,
+            )
+
+        def routed_unit(i, c):
+            acc = mm_psum.tile([P, NC], F32, name="acc")
+            for g in range(RP_):
+                routed_pass(acc, i, c, g)
+            gate_and_residual(acc, i, c)
+
+        rounded = []
+
+        def shared_unit(i, c):
+            acc = mm_psum.tile([P, NC], F32, name="acc")
+            codes, scales = hs_mx[i]
+            for g in range(SP_):
+                nc.tensor.matmul_mx(
+                    out=acc[:],
+                    lhsT=codes[:, rows(g)].bitcast(FP8X4),
+                    lhsT_scale=scales[:, rows(g)],
+                    rhs=ws_mx[c, g][0][:].bitcast(FP8X4),
+                    rhs_scale=ws_mx[c, g][1][:],
+                    start=(g == 0),
+                    stop=(g == SP_ - 1),
+                )
+            total = work.tile([P, NC], F32, name="total", bufs=3)
+            nc.vector.tensor_tensor(out=total[:], in0=acc[:], in1=partial[i, c][:], op=ADD)
+
+            def finish():
+                y = work.tile([P, NC], F32, name="y", bufs=8)
+                nc.vector.tensor_tensor(out=y[:], in0=total[:], in1=smooth_all[:, cols(c)], op=MULT)
+                nc.sync.dma_start(out=out_0[rows(i), cols(c)], in_=y[:])
+
+                def round_y():
+                    y_sorted[i, c] = work.tile([P, 2, P, 2], BF16, name="y_sorted", bufs=6)
+                    nc.scalar.copy(out=y_sorted[i, c][:], in_=y[:].rearrange("m (p u e) -> m u p e", u=2, e=2))
+                    rounded.append((clock[0], (i, c)))
+
+                defer(ROUND_DELAY, round_y)
+
+            defer(1, finish)
+
+        def turn_y(units):
+            for at in range(0, len(units), 2):
+                bank = tr_psum.tile([P, 4, P], F32, name="tr_bank")
+                pair = units[at : at + 2]
+                for n, unit in enumerate(pair):
+                    words = y_sorted[unit][:].rearrange("m u p e -> m (u p e)").bitcast(F32)
+                    for u in range(2):
+                        nc.tensor.transpose(bank[:, 2 * n + u, :], words[:, rows(u)], ident[:])
+                turned = work.tile([P, 2 * NC], BF16, name="y_turned", bufs=3, align_bytes=64)
+                unzip_bank(turned[:, : len(pair) * NC], bank, len(pair))
+                for n, (i, c) in enumerate(pair):
+
+                    def planes(turned=turned, n=n, i=i, c=c):
+                        nc.vector.quantize_mx(
+                            out=y_words[:, c, rows(i)].bitcast(FP8X4), scales=y_scales[:, c, rows(i)],
+                            in_=turned[:, cols(n)],
+                        )
+                        nc.sync.dma_start(
+                            out=out_1[c, :, rows(i), :].rearrange("p m t -> p (m t)").bitcast(I32),
+                            in_=y_words[:, c, rows(i)].bitcast(I32),
+                        )
+
+                    defer(Q_DELAY, planes)
+
+        order = [(i, c) for c in range(CHUNKS) for i in range(TILES)]
+        pace = (UNITS - LEAD) / UNITS
+        steps = [(n, "routed", u) for n, u in enumerate(order)]
+        steps = steps + [(LEAD + 0.25 + n * pace, "shared", u) for n, u in enumerate(order)]
+        steps = steps + [(i - HR_AT, "hr", i) for i in range(1, TILES)]
+        steps = steps + [(LEAD + 0.25 + i * pace - HS_AHEAD, "hs", i) for i in range(TILES)]
+        steps = sorted(steps)
+        pieces = [(c, g, h) for c in range(CHUNKS) for g in range(SP_) for h in range(W_PARTS)]
+
+        turn_h(hr_raw[0], RP_, "hr", hr_mx, 0)()
+        spread_vectors()
+        for pos, kind, arg in steps + [(UNITS + 1, "drain", 0)] * 10:
+            clock[0] = clock[0] + 1
+            ready = [unit for at, unit in rounded if at <= clock[0] - (1 if kind == "drain" else Y_AGE)]
+            if kind == "routed":
+                routed_unit(*arg)
+            elif kind == "shared":
+                shared_unit(*arg)
+            elif kind == "hr":
+                turn_h(hr_raw[arg], RP_, "hr", hr_mx, arg)()
+            elif kind == "hs":
+                turn_h(hs_raw[arg], SP_, "hs", hs_mx, arg)()
+            if ready and (kind in ("hr", "hs", "drain") or len(ready) >= Y_RUN):
+                turn_y(ready)
+                rounded[:] = [entry for entry in rounded if entry[1] not in ready]
+            due = [fn for at, fn in later if at <= clock[0]]
+            later[:] = [entry for entry in later if entry[0] > clock[0]]
+            for fn in due:
+                fn()
+            if late and pos >= LATE_AT:
+                late.pop(0)()
+            for n in range(W_RATE[0] if pieces and pieces[0][0] == 0 else W_RATE[1]):
+                if pieces and pos >= W_AT[pieces[0][0]]:
+                    group_ws(pieces.pop(0))
+        for q in range(4):
+            nc.scalar.dma_start(
+                out=out_2[:, 4 * q : 4 * q + 4, :].rearrange("g r m -> r g m").bitcast(I32),
+                in_=y_scales[32 * q : 32 * q + 4, :, :].bitcast(I32),
+            )

@@ -18,27 +18,19 @@ MULT = mybir.AluOpType.mult
 
 P = 128
 KP = 512
+WORDS = KP // 2
 NC = 512
 TILES = T // P
 CHUNKS = D // NC
 UNITS = TILES * CHUNKS
-SP_ = FS // KP
-RP_ = FR // KP
+S_PASSES = FS // KP
+R_PASSES = FR // KP
 
-LEAD = 2
-EARLY = 4
-LATE_AT = 3
-W1_AFTER = 2
-W_AT = (-3, 3, 7)
-W_ON_VECTOR = ((0, 0), (0, 1), (1, 0))
-HS_AHEAD = 1.4
-HR_AT = 1.1
-Y_RUN = 3
-Y_AGE = 3
-ROUND_DELAY = 1
-Q_DELAY = 1
-W_PARTS = 4
-W_RATE = (8, 2)
+QUARTERS = 4
+VECTOR_QUARTERS = {(0, 0): 4, (0, 1): 3, (1, 0): 2, (1, 1): 2, (2, 0): 0, (2, 1): 0}
+WARM_UP = (16, 6, 4)
+RUN = 4
+TAIL_FROM = 2 * RUN
 
 
 def tile_shared_routed_expert_merge_g5_kernel(
@@ -50,95 +42,129 @@ def tile_shared_routed_expert_merge_g5_kernel(
         work = ctx.enter_context(tc.tile_pool(name="work", bufs=2))
         mm_psum = ctx.enter_context(tc.psum_pool(name="mm_psum", bufs=4))
         tr_psum = ctx.enter_context(tc.psum_pool(name="tr_psum", bufs=4))
-        ctx.enter_context(tc.manual_schedule(engines={mybir.EngineType.PE, mybir.EngineType.SP}))
+        ctx.enter_context(tc.manual_schedule())
 
-        hr_raw, hs_raw, x_sb, ws_raw, wr_words = {}, {}, {}, {}, {}
-        hr_mx, hs_mx, ws_mx, partial, y_sorted, ws_grouped = {}, {}, {}, {}, {}, {}
+        hr_raw, hs_raw, ws_raw, x_sb, wr_words, wr_scales = {}, {}, {}, {}, {}, {}
+        hr_mx, hs_mx, ws_mx, ws_grouped = {}, {}, {}, {}
+        routed_sum, partial, total, y, y_sorted = {}, {}, {}, {}, {}
+        unit = [(i, c) for c in range(CHUNKS) for i in range(TILES)]
 
-        def rows(i):
-            return slice(i * P, (i + 1) * P)
+        def block(i, n=1):
+            return slice(i * P, (i + n) * P)
 
         def cols(c):
             return slice(c * NC, (c + 1) * NC)
 
         def load_hr(i):
             hr_raw[i] = keep.tile([P, FR], BF16, name="hr_raw%d" % i)
-            nc.sync.dma_start(out=hr_raw[i][:], in_=routed_h[rows(i), :])
+            nc.sync.dma_start(out=hr_raw[i][:], in_=routed_h[block(i), :])
 
         def load_hs(i):
             hs_raw[i] = keep.tile([P, FS], BF16, name="hs_raw%d" % i)
-            nc.sync.dma_start(out=hs_raw[i][:], in_=shared_h[rows(i), :])
+            nc.sync.dma_start(out=hs_raw[i][:], in_=shared_h[block(i), :])
 
         def load_x(i, c0, c1):
-            t = keep.tile([P, (c1 - c0) * NC], BF16, name="x_sb%d%d" % (i, c0))
-            nc.sync.dma_start(out=t[:], in_=x[rows(i), c0 * NC : c1 * NC])
+            x_part = keep.tile([P, (c1 - c0) * NC], BF16, name="x_sb%d%d" % (i, c0))
+            nc.sync.dma_start(out=x_part[:], in_=x[block(i), c0 * NC : c1 * NC])
             for c in range(c0, c1):
-                x_sb[i, c] = t[:, cols(c - c0)]
+                x_sb[i, c] = x_part[:, cols(c - c0)]
 
-        def load_wr(c):
-            wr_words[c] = keep.tile([P, RP_, 2 * NC], U8, name="wr_words%d" % c, align_bytes=64)
+        def load_ws(c, g):
+            ws_raw[c, g] = keep.tile([P, 4, NC], BF16, name="ws_raw%d%d" % (c, g))
+            src = shared_w[g * KP : (g + 1) * KP, cols(c)].rearrange("(p t) n -> p t n", t=4)
+            nc.sync.dma_start(out=ws_raw[c, g][:], in_=src)
+
+        def load_wr_words(c):
+            wr_words[c] = keep.tile([P, R_PASSES, 2 * NC], U8, name="wr_words%d" % c, align_bytes=64)
             src = routed_w_words[:, :, 2 * NC * c : 2 * NC * (c + 1)].rearrange("g p b -> p g b")
             nc.sync.dma_start(out=wr_words[c][:].bitcast(I32), in_=src.bitcast(I32))
 
         def load_wr_scales(c):
-            for q in range(4):
-                nc.sync.dma_start(
-                    out=wr_scales[c][32 * q : 32 * q + 4, :, :].bitcast(I32),
-                    in_=routed_w_scales[:, 4 * q : 4 * q + 4, cols(c)].rearrange("g r n -> r g n").bitcast(I32),
-                )
+            for quad in range(4):
+                src = routed_w_scales[:, 4 * quad : 4 * quad + 4, cols(c)].rearrange("g r n -> r g n")
+                nc.sync.dma_start(out=wr_scales[c][32 * quad : 32 * quad + 4, :, :].bitcast(I32), in_=src.bitcast(I32))
 
-        def load_ws(c, g):
-            ws_raw[c, g] = keep.tile([P, 4, NC], BF16, name="ws_raw%d%d" % (c, g))
-            src = shared_w[g * KP : (g + 1) * KP, cols(c)].rearrange("(p j) n -> p j n", j=4)
-            nc.sync.dma_start(out=ws_raw[c, g][:], in_=src)
-
-        wr_scales = {}
-        for c in range(CHUNKS):
-            wr_scales[c] = keep.tile([P, RP_, NC], U8, name="wr_scales%d" % c, align_bytes=64)
+        def zero_wr_scales(c):
             nc.vector.memset(wr_scales[c][:].rearrange("p g n -> p (g n)").bitcast(I32), 0)
+
+        ident = keep.tile([P, P], F32, name="ident")
+        warm_in = keep.tile([P, 4 * P], BF16, name="warm_in", align_bytes=64)
+        warm_codes = keep.tile([P, P], U32, name="warm_codes", align_bytes=64)
+        warm_scales = keep.tile([P, P], U8, name="warm_scales", align_bytes=64)
+        for c in range(CHUNKS):
+            wr_scales[c] = keep.tile([P, R_PASSES, NC], U8, name="wr_scales%d" % c, align_bytes=64)
+        nc.vector.memset(warm_in[:].bitcast(I32), 0)
+        zero_wr_scales(0)
+        nc.vector.quantize_mx(out=warm_codes[:].bitcast(FP8X4), scales=warm_scales[:], in_=warm_in[:])
+        nc.vector.memset(ident[:], 0.0)
+        make_identity(nc, ident[:], nomemset=True)
+        zero_wr_scales(1)
+        zero_wr_scales(2)
+
         load_hr(0)
         gate_rows = keep.tile([TILES, P], BF16, name="gate_rows")
         smooth_words = keep.tile([P, CHUNKS, 4], BF16, name="smooth_words")
-        nc.scalar.dma_start(out=gate_rows[:], in_=gate.rearrange("(i p) -> i p", p=P))
-        nc.scalar.dma_start(out=smooth_words[:], in_=smooth.rearrange("(c p t) -> p c t", c=CHUNKS, t=4))
-        ident = keep.tile([P, P], F32, name="ident")
-        make_identity(nc, ident[:])
+        nc.sync.dma_start(out=gate_rows[:], in_=gate.rearrange("(i p) -> i p", p=P))
+        nc.sync.dma_start(out=smooth_words[:], in_=smooth.rearrange("(c p t) -> p c t", c=CHUNKS, t=4))
         load_wr_scales(0)
-        load_wr(0)
+        load_wr_words(0)
         load_hr(1)
+        load_x(0, 0, 1)
+        load_hr(2)
         load_ws(0, 0)
+        load_hs(0)
+        load_hs(1)
+        load_x(1, 0, 1)
         load_ws(0, 1)
-        for i in range(TILES):
-            load_x(i, 0, 1)
-            load_hs(i)
-            if i + 2 < TILES:
-                load_hr(i + 2)
-            if i == W1_AFTER:
-                load_ws(1, 0)
-            if i == W1_AFTER + 1:
-                load_ws(1, 1)
-        late = [lambda: load_wr_scales(1), lambda: load_wr(1)]
-        late = late + [lambda: load_x(0, 1, 3), lambda: load_ws(2, 0), lambda: load_x(1, 1, 3), lambda: load_ws(2, 1)]
-        late = late + [lambda i=i: load_x(i, 1, 3) for i in range(2, TILES)]
-        late = late + [lambda: load_wr_scales(2), lambda: load_wr(2)]
-        for n in range(EARLY):
-            late.pop(0)()
+        load_hr(3)
+        load_x(2, 0, 1)
+        load_hs(2)
+        load_hr(4)
+        load_hs(3)
+        load_x(3, 0, 1)
+        load_ws(1, 0)
+        load_x(4, 0, 1)
+        load_hr(5)
+        load_hs(4)
+        load_hs(5)
+        load_ws(1, 1)
+        load_x(5, 0, 1)
+        load_wr_scales(1)
+        load_wr_words(1)
+        load_x(0, 1, CHUNKS)
+        load_x(1, 1, CHUNKS)
+        load_ws(2, 0)
+        load_x(2, 1, CHUNKS)
+        load_ws(2, 1)
+        load_x(3, 1, CHUNKS)
+        load_wr_scales(2)
+        load_x(4, 1, CHUNKS)
+        load_x(5, 1, CHUNKS)
+        load_wr_words(2)
 
         gate_pad = keep.tile([P, P], F32, name="gate_pad")
+        nc.vector.memset(gate_pad[:], 0.0)
+        nc.vector.tensor_copy(out=gate_pad[:TILES, :], in_=gate_rows[:])
         gate_col = keep.tile([P, TILES], F32, name="gate_col")
         smooth_all = keep.tile([P, D], BF16, name="smooth_all")
         y_words = keep.tile([P, CHUNKS, T], U32, name="y_words", align_bytes=64)
         y_scales = keep.tile([P, CHUNKS, T], U8, name="y_scales", align_bytes=64)
 
-        def unzip_bank(dst_bf16, bank, pairs):
-            nc.scalar.copy(
-                out=dst_bf16.bitcast(F32).rearrange("p (g r u) -> p g r u", g=pairs, u=2),
-                in_=bank[:, : 2 * pairs, :].rearrange("p (g u) r -> p g r u", u=2),
+        def warm_up(passes):
+            scratch = mm_psum.tile([P, NC], F32, name="acc")
+            for k in range(passes):
+                nc.tensor.matmul_mx(
+                    out=scratch[:, :P], lhsT=warm_codes[:].bitcast(FP8X4), lhsT_scale=warm_scales[:],
+                    rhs=warm_codes[:].bitcast(FP8X4), rhs_scale=warm_scales[:], start=True, stop=True,
+                )
+
+        def zip_bank(dst, bank, groups, copy):
+            copy(
+                out=dst.bitcast(F32).rearrange("p (g r u) -> p g r u", g=groups, u=2),
+                in_=bank[:, : 2 * groups, :].rearrange("p (g u) r -> p g r u", u=2),
             )
 
         def spread_vectors():
-            nc.vector.memset(gate_pad[:], 0.0)
-            nc.vector.tensor_copy(out=gate_pad[:TILES, :], in_=gate_rows[:])
             words = smooth_words[:].rearrange("p c t -> p (c t)").bitcast(F32)
             first = tr_psum.tile([P, 4, P], F32, name="tr_bank")
             second = tr_psum.tile([P, 4, P], F32, name="tr_bank")
@@ -147,170 +173,254 @@ def tile_shared_routed_expert_merge_g5_kernel(
                 nc.tensor.transpose(bank[:, w % 4, :], words[:, w : w + 1].to_broadcast([P, P]), ident[:])
             nc.tensor.transpose(second[:, 2, :], gate_pad[:], ident[:])
             nc.scalar.copy(out=gate_col[:], in_=second[:, 2, :TILES])
-            unzip_bank(smooth_all[:, : 2 * NC], first, 2)
-            unzip_bank(smooth_all[:, 2 * NC :], second, 1)
+            zip_bank(smooth_all[:, : 2 * NC], first, 2, nc.scalar.copy)
+            zip_bank(smooth_all[:, 2 * NC :], second, 1, nc.scalar.copy)
 
-        later = []
-        clock = [0]
+        turned_ready = []
+        weights_ready = []
 
-        def defer(steps_ahead, fn):
-            later.append((clock[0] + steps_ahead, fn))
+        def quantize(ready, count):
+            for codes, scales, values in ready[:count]:
+                nc.vector.quantize_mx(out=codes.bitcast(FP8X4), scales=scales, in_=values)
+            ready[:count] = []
 
-        def turn_h(raw, passes, tag, store, i):
+        def turn_h(raw, passes, tag, mx, i):
             words = raw[:].bitcast(F32)
-            turned = work.tile([P, passes * KP], BF16, name=tag + "_turned", align_bytes=64)
             for g0 in range(0, passes, 2):
                 bank = tr_psum.tile([P, 4, P], F32, name="tr_bank")
                 for g in range(2):
                     for u in range(2):
-                        first = 256 * (g0 + g) + u
-                        nc.tensor.transpose(bank[:, 2 * g + u, :], words[:, first : 256 * (g0 + g + 1) : 2], ident[:])
-                unzip_bank(turned[:, g0 * KP : (g0 + 2) * KP], bank, 2)
-            codes = work.tile([P, passes * P], U32, name=tag + "_codes", bufs=6, align_bytes=64)
-            scales = work.tile([P, passes * P], U8, name=tag + "_scales", bufs=6, align_bytes=64)
-            store[i] = (codes, scales)
-            return lambda: nc.vector.quantize_mx(out=codes[:].bitcast(FP8X4), scales=scales[:], in_=turned[:])
+                        every_2nd = words[:, WORDS * (g0 + g) + u : WORDS * (g0 + g + 1) : 2]
+                        nc.tensor.transpose(bank[:, 2 * g + u, :], every_2nd, ident[:])
+                turned = work.tile([P, 2 * KP], BF16, name="h_turned", bufs=4, align_bytes=64)
+                zip_bank(turned[:], bank, 2, nc.scalar.copy)
+                codes = keep.tile([P, 2 * P], U32, name="%s_codes%d%d" % (tag, i, g0), align_bytes=64)
+                scales = keep.tile([P, 2 * P], U8, name="%s_scales%d%d" % (tag, i, g0), align_bytes=64)
+                turned_ready.append((codes[:], scales[:], turned[:]))
+                for g in range(2):
+                    mx[i, g0 + g] = (codes[:, block(g)], scales[:, block(g)])
 
-        def group_ws(piece):
-            c, g, h = piece
-            if h == 0:
-                ws_grouped[c, g] = work.tile([P, NC, 4], BF16, name="ws_grouped", bufs=3, align_bytes=64)
-            grouped = ws_grouped[c, g]
-            part = slice(h * NC // W_PARTS, (h + 1) * NC // W_PARTS)
-            dst = grouped[:, part, :].rearrange("p (n i) t -> p n t i", i=4)
-            src = ws_raw[c, g][:, :, part].rearrange("p t (n i) -> p n t i", i=4)
-            if (c, g) in W_ON_VECTOR:
-                nc.vector.tensor_copy(out=dst, in_=src)
-            else:
-                nc.scalar.copy(out=dst, in_=src)
-            if h == W_PARTS - 1:
-                codes = keep.tile([P, NC], U32, name="ws_codes%d%d" % (c, g), align_bytes=64)
-                scales = keep.tile([P, NC], U8, name="ws_scales%d%d" % (c, g), align_bytes=64)
-                ws_mx[c, g] = (codes, scales)
-                defer(
-                    1,
-                    lambda: nc.vector.quantize_mx(
-                        out=codes[:].bitcast(FP8X4), scales=scales[:], in_=grouped[:].rearrange("p n t -> p (n t)")
-                    ),
+        def turn_hr(i):
+            turn_h(hr_raw[i], R_PASSES, "hr", hr_mx, i)
+
+        def turn_hs(i):
+            turn_h(hs_raw[i], S_PASSES, "hs", hs_mx, i)
+
+        ws_quarters = [(c, g, h) for c in range(CHUNKS) for g in range(S_PASSES) for h in range(QUARTERS)]
+
+        def group_ws(count):
+            for c, g, h in ws_quarters[:count]:
+                if h == 0:
+                    ws_grouped[c, g] = work.tile([P, NC, 4], BF16, name="ws_grouped", align_bytes=64)
+                quarter = slice(h * NC // QUARTERS, (h + 1) * NC // QUARTERS)
+                copy = nc.vector.tensor_copy if h < VECTOR_QUARTERS[c, g] else nc.scalar.copy
+                copy(
+                    out=ws_grouped[c, g][:, quarter, :].rearrange("p (n i) t -> p n t i", i=4),
+                    in_=ws_raw[c, g][:, :, quarter].rearrange("p t (n i) -> p n t i", i=4),
                 )
+                if h == QUARTERS - 1:
+                    codes = keep.tile([P, NC], U32, name="ws_codes%d%d" % (c, g), align_bytes=64)
+                    scales = keep.tile([P, NC], U8, name="ws_scales%d%d" % (c, g), align_bytes=64)
+                    ws_mx[c, g] = (codes, scales)
+                    weights_ready.append((codes[:], scales[:], ws_grouped[c, g][:].rearrange("p n t -> p (n t)")))
+            ws_quarters[:count] = []
 
-        def routed_pass(acc, i, c, g):
-            codes, scales = hr_mx[i]
-            nc.tensor.matmul_mx(
-                out=acc[:],
-                lhsT=codes[:, rows(g)].bitcast(FP8X4),
-                lhsT_scale=scales[:, rows(g)],
-                rhs=wr_words[c][:, g, :].bitcast(FP4X4),
-                rhs_scale=wr_scales[c][:, g, :],
-                start=(g == 0),
-                stop=(g == RP_ - 1),
-            )
-
-        def gate_and_residual(acc, i, c):
-            partial[i, c] = work.tile([P, NC], F32, name="partial", bufs=5)
-            nc.vector.scalar_tensor_tensor(
-                out=partial[i, c][:], in0=acc[:], scalar=gate_col[:, i : i + 1], in1=x_sb[i, c],
-                op0=MULT, op1=ADD,
-            )
-
-        def routed_unit(i, c):
-            acc = mm_psum.tile([P, NC], F32, name="acc")
-            for g in range(RP_):
-                routed_pass(acc, i, c, g)
-            gate_and_residual(acc, i, c)
-
-        rounded = []
-
-        def shared_unit(i, c):
-            acc = mm_psum.tile([P, NC], F32, name="acc")
-            codes, scales = hs_mx[i]
-            for g in range(SP_):
+        def routed_matmuls(n):
+            i, c = unit[n]
+            routed_sum[n] = mm_psum.tile([P, NC], F32, name="acc")
+            for g in range(R_PASSES):
                 nc.tensor.matmul_mx(
-                    out=acc[:],
-                    lhsT=codes[:, rows(g)].bitcast(FP8X4),
-                    lhsT_scale=scales[:, rows(g)],
-                    rhs=ws_mx[c, g][0][:].bitcast(FP8X4),
-                    rhs_scale=ws_mx[c, g][1][:],
-                    start=(g == 0),
-                    stop=(g == SP_ - 1),
+                    out=routed_sum[n][:], lhsT=hr_mx[i, g][0].bitcast(FP8X4), lhsT_scale=hr_mx[i, g][1],
+                    rhs=wr_words[c][:, g, :].bitcast(FP4X4), rhs_scale=wr_scales[c][:, g, :],
+                    start=(g == 0), stop=(g == R_PASSES - 1),
                 )
-            total = work.tile([P, NC], F32, name="total", bufs=3)
-            nc.vector.tensor_tensor(out=total[:], in0=acc[:], in1=partial[i, c][:], op=ADD)
 
-            def finish():
-                y = work.tile([P, NC], F32, name="y", bufs=8)
-                nc.vector.tensor_tensor(out=y[:], in0=total[:], in1=smooth_all[:, cols(c)], op=MULT)
-                nc.sync.dma_start(out=out_0[rows(i), cols(c)], in_=y[:])
+        def shared_matmuls(n):
+            i, c = unit[n]
+            shared_sum = mm_psum.tile([P, NC], F32, name="acc")
+            for g in range(S_PASSES):
+                nc.tensor.matmul_mx(
+                    out=shared_sum[:], lhsT=hs_mx[i, g][0].bitcast(FP8X4), lhsT_scale=hs_mx[i, g][1],
+                    rhs=ws_mx[c, g][0][:].bitcast(FP8X4), rhs_scale=ws_mx[c, g][1][:],
+                    start=(g == 0), stop=(g == S_PASSES - 1),
+                )
+            return shared_sum
 
-                def round_y():
-                    y_sorted[i, c] = work.tile([P, 2, P, 2], BF16, name="y_sorted", bufs=6)
-                    nc.scalar.copy(out=y_sorted[i, c][:], in_=y[:].rearrange("m (p u e) -> m u p e", u=2, e=2))
-                    rounded.append((clock[0], (i, c)))
+        whole = [slice(0, NC)]
+        halves = [slice(0, NC // 2), slice(NC // 2, NC)]
 
-                defer(ROUND_DELAY, round_y)
+        def gate_and_residual(n, parts=whole):
+            i, c = unit[n]
+            partial[n] = work.tile([P, NC], F32, name="partial", bufs=5)
+            for s in parts:
+                nc.vector.scalar_tensor_tensor(
+                    out=partial[n][:, s], in0=routed_sum[n][:, s], scalar=gate_col[:, i : i + 1],
+                    in1=x_sb[i, c][:, s], op0=MULT, op1=ADD,
+                )
 
-            defer(1, finish)
+        def add_shared(n, shared_sum, parts=whole):
+            total[n] = work.tile([P, NC], F32, name="total", bufs=4)
+            for s in parts:
+                nc.vector.tensor_tensor(out=total[n][:, s], in0=shared_sum[:, s], in1=partial[n][:, s], op=ADD)
 
-        def turn_y(units):
-            for at in range(0, len(units), 2):
-                bank = tr_psum.tile([P, 4, P], F32, name="tr_bank")
-                pair = units[at : at + 2]
-                for n, unit in enumerate(pair):
-                    words = y_sorted[unit][:].rearrange("m u p e -> m (u p e)").bitcast(F32)
-                    for u in range(2):
-                        nc.tensor.transpose(bank[:, 2 * n + u, :], words[:, rows(u)], ident[:])
-                turned = work.tile([P, 2 * NC], BF16, name="y_turned", bufs=3, align_bytes=64)
-                unzip_bank(turned[:, : len(pair) * NC], bank, len(pair))
-                for n, (i, c) in enumerate(pair):
+        def routed_unit(n):
+            routed_matmuls(n)
+            gate_and_residual(n)
 
-                    def planes(turned=turned, n=n, i=i, c=c):
-                        nc.vector.quantize_mx(
-                            out=y_words[:, c, rows(i)].bitcast(FP8X4), scales=y_scales[:, c, rows(i)],
-                            in_=turned[:, cols(n)],
-                        )
-                        nc.sync.dma_start(
-                            out=out_1[c, :, rows(i), :].rearrange("p m t -> p (m t)").bitcast(I32),
-                            in_=y_words[:, c, rows(i)].bitcast(I32),
-                        )
+        def shared_unit(n):
+            add_shared(n, shared_matmuls(n))
 
-                    defer(Q_DELAY, planes)
+        def scale_y(n, engine, parts=whole):
+            y[n] = work.tile([P, NC], F32, name="y", bufs=9)
+            for s in parts:
+                engine.tensor_tensor(
+                    out=y[n][:, s], in0=total[n][:, s], in1=smooth_all[:, cols(unit[n][1])][:, s], op=MULT
+                )
 
-        order = [(i, c) for c in range(CHUNKS) for i in range(TILES)]
-        pace = (UNITS - LEAD) / UNITS
-        steps = [(n, "routed", u) for n, u in enumerate(order)]
-        steps = steps + [(LEAD + 0.25 + n * pace, "shared", u) for n, u in enumerate(order)]
-        steps = steps + [(i - HR_AT, "hr", i) for i in range(1, TILES)]
-        steps = steps + [(LEAD + 0.25 + i * pace - HS_AHEAD, "hs", i) for i in range(TILES)]
-        steps = sorted(steps)
-        pieces = [(c, g, h) for c in range(CHUNKS) for g in range(SP_) for h in range(W_PARTS)]
+        def store_y(n):
+            i, c = unit[n]
+            nc.sync.dma_start(out=out_0[block(i), cols(c)], in_=y[n][:])
 
-        turn_h(hr_raw[0], RP_, "hr", hr_mx, 0)()
+        def round_y(n, parts=whole):
+            y_sorted[n] = work.tile([P, 2, P, 2], BF16, name="y_sorted", bufs=UNITS - TAIL_FROM)
+            for s in parts:
+                nc.scalar.copy(
+                    out=y_sorted[n][:, :, s.start // 4 : s.stop // 4, :],
+                    in_=y[n][:, s].rearrange("m (p u e) -> m u p e", u=2, e=2),
+                )
+
+        def turn_y(n, count, copy):
+            i, c = unit[n]
+            bank = tr_psum.tile([P, 4, P], F32, name="tr_bank")
+            for j in range(count):
+                words = y_sorted[n + j][:].rearrange("m u p e -> m (u p e)").bitcast(F32)
+                for u in range(2):
+                    nc.tensor.transpose(bank[:, 2 * j + u, :], words[:, block(u)], ident[:])
+            turned = work.tile([P, 2 * NC], BF16, name="y_turned", bufs=5, align_bytes=64)
+            zip_bank(turned[:, : count * NC], bank, count, copy)
+            tokens = block(i, count)
+            turned_ready.append((y_words[:, c, tokens], y_scales[:, c, tokens], turned[:, : count * NC]))
+
+        def store_words(n0, n1):
+            for c in sorted(set(unit[n][1] for n in range(n0, n1))):
+                tiles = [unit[n][0] for n in range(n0, n1) if unit[n][1] == c]
+                tokens = block(tiles[0], len(tiles))
+                nc.sync.dma_start(
+                    out=out_1[c, :, tokens, :].rearrange("p m t -> p (m t)").bitcast(I32),
+                    in_=y_words[:, c, tokens].bitcast(I32),
+                )
+
+        def store_scales(c0, c1, second_queue):
+            for quad in range(4):
+                queue = second_queue if quad % 2 else nc.sync
+                queue.dma_start(
+                    out=out_2[c0:c1, 4 * quad : 4 * quad + 4, :].rearrange("g r m -> r g m").bitcast(I32),
+                    in_=y_scales[32 * quad : 32 * quad + 4, c0:c1, :].bitcast(I32),
+                )
+
+        warm_up(WARM_UP[0])
+        turn_hr(0)
+        quantize(turned_ready, 2)
         spread_vectors()
-        for pos, kind, arg in steps + [(UNITS + 1, "drain", 0)] * 10:
-            clock[0] = clock[0] + 1
-            ready = [unit for at, unit in rounded if at <= clock[0] - (1 if kind == "drain" else Y_AGE)]
-            if kind == "routed":
-                routed_unit(*arg)
-            elif kind == "shared":
-                shared_unit(*arg)
-            elif kind == "hr":
-                turn_h(hr_raw[arg], RP_, "hr", hr_mx, arg)()
-            elif kind == "hs":
-                turn_h(hs_raw[arg], SP_, "hs", hs_mx, arg)()
-            if ready and (kind in ("hr", "hs", "drain") or len(ready) >= Y_RUN):
-                turn_y(ready)
-                rounded[:] = [entry for entry in rounded if entry[1] not in ready]
-            due = [fn for at, fn in later if at <= clock[0]]
-            later[:] = [entry for entry in later if entry[0] > clock[0]]
-            for fn in due:
-                fn()
-            if late and pos >= LATE_AT:
-                late.pop(0)()
-            for n in range(W_RATE[0] if pieces and pieces[0][0] == 0 else W_RATE[1]):
-                if pieces and pos >= W_AT[pieces[0][0]]:
-                    group_ws(pieces.pop(0))
-        for q in range(4):
-            nc.scalar.dma_start(
-                out=out_2[:, 4 * q : 4 * q + 4, :].rearrange("g r m -> r g m").bitcast(I32),
-                in_=y_scales[32 * q : 32 * q + 4, :, :].bitcast(I32),
-            )
+        warm_up(WARM_UP[1])
+        routed_matmuls(0)
+        turn_hr(1)
+        gate_and_residual(0)
+        quantize(turned_ready, 2)
+        warm_up(WARM_UP[2])
+        turn_hr(2)
+        group_ws(3)
+        quantize(turned_ready, 1)
+        group_ws(1)
+        quantize(turned_ready, 1)
+        routed_matmuls(1)
+        quantize(weights_ready, 1)
+        turn_hs(0)
+        turn_hs(1)
+        group_ws(QUARTERS)
+        quantize(turned_ready, 1)
+        routed_matmuls(2)
+        quantize(weights_ready, 1)
+        gate_and_residual(1)
+        quantize(turned_ready, 1)
+        turn_hr(3)
+        gate_and_residual(2)
+        quantize(turned_ready, 1)
+        shared_unit(0)
+        quantize(turned_ready, 1)
+        scale_y(0, nc.vector)
+        shared_unit(1)
+
+        for i in range(3, TILES):
+            is_last = i == TILES - 1
+            turn_hs(i - 1)
+            if is_last:
+                turn_hs(i)
+                round_y(i - 3)
+                quantize(weights_ready, 1)
+            else:
+                turn_hr(i + 1)
+            quantize(turned_ready, 1)
+            scale_y(i - 2, nc.vector)
+            if i == 3:
+                round_y(0)
+            if i != 4:
+                round_y(i - 2)
+            quantize(turned_ready, 1)
+            routed_unit(i)
+            quantize(turned_ready, 1)
+            group_ws(QUARTERS if is_last else QUARTERS // 2)
+            shared_unit(i - 1)
+        quantize(weights_ready, 1)
+        for n in range(3):
+            store_y(n)
+
+        last = UNITS - 1
+        for n in range(TILES, last):
+            routed_unit(n)
+            if n - 2 not in y:
+                scale_y(n - 2, nc.vector)
+                quantize(turned_ready, RUN // 2)
+                quantize(weights_ready, 1)
+            shared_unit(n - 1)
+            if n % 2 == 1:
+                scale_y(n - 1, nc.gpsimd)
+            if n - 3 not in y_sorted:
+                round_y(n - 3)
+            store_y(n - 3)
+            if n % RUN == RUN - 1 and n - 3 <= TAIL_FROM:
+                for m in range(n - 3 - RUN, n - 3, 2):
+                    turn_y(m, 2, nc.scalar.copy)
+            if n % RUN == 2 and RUN <= n - 6 <= TAIL_FROM:
+                store_words(n - 6 - RUN, n - 6)
+                if n - 6 >= TILES:
+                    store_scales(0, 1, nc.sync)
+            group_ws(QUARTERS // 2)
+
+        shared_unit(last - 1)
+        scale_y(last - 2, nc.vector)
+        scale_y(last - 1, nc.gpsimd)
+        for n in (last - 3, last - 2):
+            round_y(n)
+            store_y(n)
+        routed_matmuls(last)
+        shared_last = shared_matmuls(last)
+        gate_and_residual(last, halves)
+        add_shared(last, shared_last, halves)
+        scale_y(last, nc.vector, halves)
+        turn_y(TAIL_FROM, 2, nc.scalar.copy)
+        round_y(last - 1)
+        store_y(last - 1)
+        round_y(last, halves)
+        store_y(last)
+        for n in range(TAIL_FROM + 2, last - 1, 2):
+            turn_y(n, 2, nc.vector.tensor_copy if n < last - 3 else nc.scalar.copy)
+            quantize(turned_ready, 1)
+            store_words(n - 2, n)
+        quantize(turned_ready, 1)
+        store_words(last - 3, last - 1)
+        turn_y(last - 1, 1, nc.scalar.copy)
+        turn_y(last, 1, nc.scalar.copy)
+        quantize(turned_ready, 2)
+        store_words(last - 1, UNITS)
+        store_scales(1, CHUNKS, nc.scalar)

@@ -27,7 +27,7 @@ S_PASSES = FS // KP
 R_PASSES = FR // KP
 
 QUARTERS = 4
-VECTOR_QUARTERS = {(0, 0): 4, (0, 1): 3, (1, 0): 2, (1, 1): 2, (2, 0): 0, (2, 1): 0}
+VECTOR_QUARTERS = {(0, 0): 3, (0, 1): 3, (1, 0): 2, (1, 1): 2, (2, 0): 0, (2, 1): 0}
 WARM_UP = (16, 6, 4)
 RUN = 4
 TAIL_FROM = 2 * RUN
@@ -122,10 +122,10 @@ def tile_shared_routed_expert_merge_g5_kernel(
         load_hr(4)
         load_hs(3)
         load_x(3, 0, 1)
-        load_ws(1, 0)
-        load_x(4, 0, 1)
         load_hr(5)
         load_hs(4)
+        load_ws(1, 0)
+        load_x(4, 0, 1)
         load_hs(5)
         load_ws(1, 1)
         load_x(5, 0, 1)
@@ -184,14 +184,24 @@ def tile_shared_routed_expert_merge_g5_kernel(
                 nc.vector.quantize_mx(out=codes.bitcast(FP8X4), scales=scales, in_=values)
             ready[:count] = []
 
+        sorted_words = {}
+
+        def sort_h(raw, passes, tag, i, bufs):
+            packed = work.tile([P, passes, 2, P], F32, name=tag + "_sorted", bufs=bufs)
+            nc.scalar.copy(out=packed[:], in_=raw[:].bitcast(F32).rearrange("m (g p u) -> m g u p", g=passes, u=2))
+            sorted_words[tag, i] = packed
+
         def turn_h(raw, passes, tag, mx, i):
             words = raw[:].bitcast(F32)
             for g0 in range(0, passes, 2):
                 bank = tr_psum.tile([P, 4, P], F32, name="tr_bank")
-                for g in range(2):
+                for g in range(g0, g0 + 2):
                     for u in range(2):
-                        every_2nd = words[:, WORDS * (g0 + g) + u : WORDS * (g0 + g + 1) : 2]
-                        nc.tensor.transpose(bank[:, 2 * g + u, :], every_2nd, ident[:])
+                        if (tag, i) in sorted_words:
+                            every_2nd = sorted_words[tag, i][:, g, u, :]
+                        else:
+                            every_2nd = words[:, WORDS * g + u : WORDS * (g + 1) : 2]
+                        nc.tensor.transpose(bank[:, 2 * (g - g0) + u, :], every_2nd, ident[:])
                 turned = work.tile([P, 2 * KP], BF16, name="h_turned", bufs=4, align_bytes=64)
                 zip_bank(turned[:], bank, 2, nc.scalar.copy)
                 codes = keep.tile([P, 2 * P], U32, name="%s_codes%d%d" % (tag, i, g0), align_bytes=64)
@@ -329,21 +339,21 @@ def tile_shared_routed_expert_merge_g5_kernel(
         quantize(turned_ready, 2)
         warm_up(WARM_UP[2])
         turn_hr(2)
-        group_ws(3)
+        group_ws(QUARTERS // 2)
         quantize(turned_ready, 1)
-        group_ws(1)
+        group_ws(QUARTERS // 2)
         quantize(turned_ready, 1)
-        routed_matmuls(1)
-        quantize(weights_ready, 1)
+        routed_unit(1)
         turn_hs(0)
         turn_hs(1)
+        quantize(weights_ready, 1)
         group_ws(QUARTERS)
         quantize(turned_ready, 1)
         routed_matmuls(2)
         quantize(weights_ready, 1)
-        gate_and_residual(1)
         quantize(turned_ready, 1)
         turn_hr(3)
+        sort_h(hs_raw[3], S_PASSES, "hs", 3, 2)
         gate_and_residual(2)
         quantize(turned_ready, 1)
         shared_unit(0)
@@ -351,27 +361,39 @@ def tile_shared_routed_expert_merge_g5_kernel(
         scale_y(0, nc.vector)
         shared_unit(1)
 
-        for i in range(3, TILES):
-            is_last = i == TILES - 1
-            turn_hs(i - 1)
-            if is_last:
-                turn_hs(i)
-                round_y(i - 3)
-                quantize(weights_ready, 1)
-            else:
-                turn_hr(i + 1)
-            quantize(turned_ready, 1)
-            scale_y(i - 2, nc.vector)
-            if i == 3:
-                round_y(0)
-            if i != 4:
-                round_y(i - 2)
-            quantize(turned_ready, 1)
-            routed_unit(i)
-            quantize(turned_ready, 1)
-            group_ws(QUARTERS if is_last else QUARTERS // 2)
-            shared_unit(i - 1)
+        turn_hs(2)
+        turn_hr(4)
+        quantize(turned_ready, 1)
+        scale_y(1, nc.vector)
+        sort_h(hr_raw[5], R_PASSES, "hr", 5, 1)
+        sort_h(hs_raw[4], S_PASSES, "hs", 4, 2)
+        quantize(turned_ready, 1)
+        routed_unit(3)
+        quantize(turned_ready, 1)
+        group_ws(QUARTERS // 2)
+        shared_unit(2)
+
+        turn_hs(3)
+        turn_hr(5)
+        turn_hs(4)
+        quantize(turned_ready, 1)
+        scale_y(2, nc.vector)
+        quantize(turned_ready, 1)
+        routed_unit(4)
+        quantize(turned_ready, 2)
+        group_ws(QUARTERS // 2)
+        shared_unit(3)
+
+        turn_hs(5)
         quantize(weights_ready, 1)
+        scale_y(3, nc.vector)
+        routed_unit(5)
+        quantize(turned_ready, 1)
+        group_ws(QUARTERS)
+        shared_unit(4)
+        quantize(weights_ready, 1)
+        for n in range(RUN):
+            round_y(n)
         for n in range(3):
             store_y(n)
 

@@ -28,7 +28,6 @@ R_PASSES = FR // KP
 
 QUARTERS = 4
 VECTOR_QUARTERS = {(0, 0): 3, (0, 1): 3, (1, 0): 2, (1, 1): 2, (2, 0): 0, (2, 1): 0}
-WARM_UP = (16, 6, 4)
 RUN = 4
 TAIL_FROM = 2 * RUN
 
@@ -88,14 +87,9 @@ def tile_shared_routed_expert_merge_g5_kernel(
             nc.vector.memset(wr_scales[c][:].rearrange("p g n -> p (g n)").bitcast(I32), 0)
 
         ident = keep.tile([P, P], F32, name="ident")
-        warm_in = keep.tile([P, 4 * P], BF16, name="warm_in", align_bytes=64)
-        warm_codes = keep.tile([P, P], U32, name="warm_codes", align_bytes=64)
-        warm_scales = keep.tile([P, P], U8, name="warm_scales", align_bytes=64)
         for c in range(CHUNKS):
             wr_scales[c] = keep.tile([P, R_PASSES, NC], U8, name="wr_scales%d" % c, align_bytes=64)
-        nc.vector.memset(warm_in[:].bitcast(I32), 0)
         zero_wr_scales(0)
-        nc.vector.quantize_mx(out=warm_codes[:].bitcast(FP8X4), scales=warm_scales[:], in_=warm_in[:])
         nc.vector.memset(ident[:], 0.0)
         make_identity(nc, ident[:], nomemset=True)
         zero_wr_scales(1)
@@ -149,14 +143,6 @@ def tile_shared_routed_expert_merge_g5_kernel(
         smooth_all = keep.tile([P, D], BF16, name="smooth_all")
         y_words = keep.tile([P, CHUNKS, T], U32, name="y_words", align_bytes=64)
         y_scales = keep.tile([P, CHUNKS, T], U8, name="y_scales", align_bytes=64)
-
-        def warm_up(passes):
-            scratch = mm_psum.tile([P, NC], F32, name="acc")
-            for k in range(passes):
-                nc.tensor.matmul_mx(
-                    out=scratch[:, :P], lhsT=warm_codes[:].bitcast(FP8X4), lhsT_scale=warm_scales[:],
-                    rhs=warm_codes[:].bitcast(FP8X4), rhs_scale=warm_scales[:], start=True, stop=True,
-                )
 
         def zip_bank(dst, bank, groups, copy):
             copy(
@@ -328,16 +314,13 @@ def tile_shared_routed_expert_merge_g5_kernel(
                     in_=y_scales[32 * quad : 32 * quad + 4, c0:c1, :].bitcast(I32),
                 )
 
-        warm_up(WARM_UP[0])
         turn_hr(0)
         quantize(turned_ready, 2)
         spread_vectors()
-        warm_up(WARM_UP[1])
         routed_matmuls(0)
         turn_hr(1)
         gate_and_residual(0)
         quantize(turned_ready, 2)
-        warm_up(WARM_UP[2])
         turn_hr(2)
         group_ws(QUARTERS // 2)
         quantize(turned_ready, 1)

from contextlib import ExitStack

import concourse.mybir as mybir
from concourse.masks import make_identity

T, FS, FR, D = 768, 1024, 2048, 1536
FLOPS = 2 * T * (FS + FR) * D

F32 = mybir.dt.float32
BF16 = mybir.dt.bfloat16
I32 = mybir.dt.int32
U32 = mybir.dt.uint32
U8 = mybir.dt.uint8
FP8X4 = mybir.dt.float8_e4m3fn_x4
FP4X4 = mybir.dt.float4_e2m1fn_x4
ADD = mybir.AluOpType.add
MULT = mybir.AluOpType.mult

P = 128
KP = 512
WORDS = KP // 2
NC = 512
TILES = T // P
CHUNKS = D // NC
UNITS = TILES * CHUNKS
S_PASSES = FS // KP
R_PASSES = FR // KP

QUARTERS = 4
VECTOR_QUARTERS = {(0, 0): 3, (0, 1): 3, (1, 0): 2, (1, 1): 2, (2, 0): 0, (2, 1): 0}
RUN = 4
TAIL_FROM = 2 * RUN


def tile_shared_routed_expert_merge_g5_kernel(
    tc, shared_h, shared_w, routed_h, routed_w_words, routed_w_scales, gate, x, smooth, out_0, out_1, out_2
):
    nc = tc.nc
    with ExitStack() as ctx:
        keep = ctx.enter_context(tc.tile_pool(name="keep", bufs=1))
        work = ctx.enter_context(tc.tile_pool(name="work", bufs=2))
        mm_psum = ctx.enter_context(tc.psum_pool(name="mm_psum", bufs=4))
        tr_psum = ctx.enter_context(tc.psum_pool(name="tr_psum", bufs=4))
        ctx.enter_context(tc.manual_schedule())

        hr_raw, hs_raw, ws_raw, x_sb, wr_words, wr_scales = {}, {}, {}, {}, {}, {}
        hr_mx, hs_mx, ws_mx, ws_grouped = {}, {}, {}, {}
        routed_sum, partial, total, y, y_sorted = {}, {}, {}, {}, {}
        unit = [(i, c) for c in range(CHUNKS) for i in range(TILES)]

        def block(i, n=1):
            return slice(i * P, (i + n) * P)

        def cols(c):
            return slice(c * NC, (c + 1) * NC)

        def load_hr(i):
            hr_raw[i] = keep.tile([P, FR], BF16, name="hr_raw%d" % i)
            nc.sync.dma_start(out=hr_raw[i][:], in_=routed_h[block(i), :])

        def load_hs(i):
            hs_raw[i] = keep.tile([P, FS], BF16, name="hs_raw%d" % i)
            nc.sync.dma_start(out=hs_raw[i][:], in_=shared_h[block(i), :])

        def load_x(i, c0, c1):
            x_part = keep.tile([P, (c1 - c0) * NC], BF16, name="x_sb%d%d" % (i, c0))
            nc.sync.dma_start(out=x_part[:], in_=x[block(i), c0 * NC : c1 * NC])
            for c in range(c0, c1):
                x_sb[i, c] = x_part[:, cols(c - c0)]

        def load_ws(c, g):
            ws_raw[c, g] = keep.tile([P, 4, NC], BF16, name="ws_raw%d%d" % (c, g))
            src = shared_w[g * KP : (g + 1) * KP, cols(c)].rearrange("(p t) n -> p t n", t=4)
            nc.sync.dma_start(out=ws_raw[c, g][:], in_=src)

        def load_wr_words(c):
            wr_words[c] = keep.tile([P, R_PASSES, 2 * NC], U8, name="wr_words%d" % c, align_bytes=64)
            src = routed_w_words[:, :, 2 * NC * c : 2 * NC * (c + 1)].rearrange("g p b -> p g b")
            nc.sync.dma_start(out=wr_words[c][:].bitcast(I32), in_=src.bitcast(I32))

        def load_wr_scales(c):
            for quad in range(4):
                src = routed_w_scales[:, 4 * quad : 4 * quad + 4, cols(c)].rearrange("g r n -> r g n")
                nc.sync.dma_start(out=wr_scales[c][32 * quad : 32 * quad + 4, :, :].bitcast(I32), in_=src.bitcast(I32))

        def zero_wr_scales(c):
            nc.vector.memset(wr_scales[c][:].rearrange("p g n -> p (g n)").bitcast(I32), 0)

        ident = keep.tile([P, P], F32, name="ident")
        for c in range(CHUNKS):
            wr_scales[c] = keep.tile([P, R_PASSES, NC], U8, name="wr_scales%d" % c, align_bytes=64)
        zero_wr_scales(0)
        nc.vector.memset(ident[:], 0.0)
        make_identity(nc, ident[:], nomemset=True)
        zero_wr_scales(1)
        zero_wr_scales(2)

        load_hr(0)
        gate_rows = keep.tile([TILES, P], BF16, name="gate_rows")
        smooth_words = keep.tile([P, CHUNKS, 4], BF16, name="smooth_words")
        nc.sync.dma_start(out=gate_rows[:], in_=gate.rearrange("(i p) -> i p", p=P))
        nc.sync.dma_start(out=smooth_words[:], in_=smooth.rearrange("(c p t) -> p c t", c=CHUNKS, t=4))
        load_wr_scales(0)
        load_wr_words(0)
        load_hr(1)
        load_x(0, 0, 1)
        load_hr(2)
        load_ws(0, 0)
        load_hs(0)
        load_hs(1)
        load_x(1, 0, 1)
        load_ws(0, 1)
        load_hr(3)
        load_x(2, 0, 1)
        load_hs(2)
        load_hr(4)
        load_hs(3)
        load_x(3, 0, 1)
        load_hr(5)
        load_hs(4)
        load_ws(1, 0)
        load_x(4, 0, 1)
        load_hs(5)
        load_ws(1, 1)
        load_x(5, 0, 1)
        load_wr_scales(1)
        load_wr_words(1)
        load_x(0, 1, CHUNKS)
        load_x(1, 1, CHUNKS)
        load_ws(2, 0)
        load_x(2, 1, CHUNKS)
        load_ws(2, 1)
        load_x(3, 1, CHUNKS)
        load_wr_scales(2)
        load_x(4, 1, CHUNKS)
        load_x(5, 1, CHUNKS)
        load_wr_words(2)

        gate_pad = keep.tile([P, P], F32, name="gate_pad")
        nc.vector.memset(gate_pad[:], 0.0)
        nc.vector.tensor_copy(out=gate_pad[:TILES, :], in_=gate_rows[:])
        gate_col = keep.tile([P, TILES], F32, name="gate_col")
        smooth_all = keep.tile([P, D], BF16, name="smooth_all")
        y_words = keep.tile([P, CHUNKS, T], U32, name="y_words", align_bytes=64)
        y_scales = keep.tile([P, CHUNKS, T], U8, name="y_scales", align_bytes=64)

        def zip_bank(dst, bank, groups, copy):
            copy(
                out=dst.bitcast(F32).rearrange("p (g r u) -> p g r u", g=groups, u=2),
                in_=bank[:, : 2 * groups, :].rearrange("p (g u) r -> p g r u", u=2),
            )

        def spread_vectors():
            words = smooth_words[:].rearrange("p c t -> p (c t)").bitcast(F32)
            first = tr_psum.tile([P, 4, P], F32, name="tr_bank")
            second = tr_psum.tile([P, 4, P], F32, name="tr_bank")
            for w in range(2 * CHUNKS):
                bank = first if w < 4 else second
                nc.tensor.transpose(bank[:, w % 4, :], words[:, w : w + 1].to_broadcast([P, P]), ident[:])
            nc.tensor.transpose(second[:, 2, :], gate_pad[:], ident[:])
            nc.scalar.copy(out=gate_col[:], in_=second[:, 2, :TILES])
            zip_bank(smooth_all[:, : 2 * NC], first, 2, nc.scalar.copy)
            zip_bank(smooth_all[:, 2 * NC :], second, 1, nc.scalar.copy)

        turned_ready = []
        weights_ready = []

        def quantize(ready, count):
            for codes, scales, values in ready[:count]:
                nc.vector.quantize_mx(out=codes.bitcast(FP8X4), scales=scales, in_=values)
            ready[:count] = []

        sorted_words = {}

        def sort_h(raw, passes, tag, i, bufs):
            packed = work.tile([P, passes, 2, P], F32, name=tag + "_sorted", bufs=bufs)
            nc.scalar.copy(out=packed[:], in_=raw[:].bitcast(F32).rearrange("m (g p u) -> m g u p", g=passes, u=2))
            sorted_words[tag, i] = packed

        def turn_h(raw, passes, tag, mx, i):
            words = raw[:].bitcast(F32)
            for g0 in range(0, passes, 2):
                bank = tr_psum.tile([P, 4, P], F32, name="tr_bank")
                for g in range(g0, g0 + 2):
                    for u in range(2):
                        if (tag, i) in sorted_words:
                            every_2nd = sorted_words[tag, i][:, g, u, :]
                        else:
                            every_2nd = words[:, WORDS * g + u : WORDS * (g + 1) : 2]
                        nc.tensor.transpose(bank[:, 2 * (g - g0) + u, :], every_2nd, ident[:])
                turned = work.tile([P, 2 * KP], BF16, name="h_turned", bufs=4, align_bytes=64)
                zip_bank(turned[:], bank, 2, nc.scalar.copy)
                codes = keep.tile([P, 2 * P], U32, name="%s_codes%d%d" % (tag, i, g0), align_bytes=64)
                scales = keep.tile([P, 2 * P], U8, name="%s_scales%d%d" % (tag, i, g0), align_bytes=64)
                turned_ready.append((codes[:], scales[:], turned[:]))
                for g in range(2):
                    mx[i, g0 + g] = (codes[:, block(g)], scales[:, block(g)])

        def turn_hr(i):
            turn_h(hr_raw[i], R_PASSES, "hr", hr_mx, i)

        def turn_hs(i):
            turn_h(hs_raw[i], S_PASSES, "hs", hs_mx, i)

        ws_quarters = [(c, g, h) for c in range(CHUNKS) for g in range(S_PASSES) for h in range(QUARTERS)]

        def group_ws(count):
            for c, g, h in ws_quarters[:count]:
                if h == 0:
                    ws_grouped[c, g] = work.tile([P, NC, 4], BF16, name="ws_grouped", align_bytes=64)
                quarter = slice(h * NC // QUARTERS, (h + 1) * NC // QUARTERS)
                copy = nc.vector.tensor_copy if h < VECTOR_QUARTERS[c, g] else nc.scalar.copy
                copy(
                    out=ws_grouped[c, g][:, quarter, :].rearrange("p (n i) t -> p n t i", i=4),
                    in_=ws_raw[c, g][:, :, quarter].rearrange("p t (n i) -> p n t i", i=4),
                )
                if h == QUARTERS - 1:
                    codes = keep.tile([P, NC], U32, name="ws_codes%d%d" % (c, g), align_bytes=64)
                    scales = keep.tile([P, NC], U8, name="ws_scales%d%d" % (c, g), align_bytes=64)
                    ws_mx[c, g] = (codes, scales)
                    weights_ready.append((codes[:], scales[:], ws_grouped[c, g][:].rearrange("p n t -> p (n t)")))
            ws_quarters[:count] = []

        def routed_matmuls(n):
            i, c = unit[n]
            routed_sum[n] = mm_psum.tile([P, NC], F32, name="acc")
            for g in range(R_PASSES):
                nc.tensor.matmul_mx(
                    out=routed_sum[n][:], lhsT=hr_mx[i, g][0].bitcast(FP8X4), lhsT_scale=hr_mx[i, g][1],
                    rhs=wr_words[c][:, g, :].bitcast(FP4X4), rhs_scale=wr_scales[c][:, g, :],
                    start=(g == 0), stop=(g == R_PASSES - 1),
                )

        def shared_matmuls(n):
            i, c = unit[n]
            shared_sum = mm_psum.tile([P, NC], F32, name="acc")
            for g in range(S_PASSES):
                nc.tensor.matmul_mx(
                    out=shared_sum[:], lhsT=hs_mx[i, g][0].bitcast(FP8X4), lhsT_scale=hs_mx[i, g][1],
                    rhs=ws_mx[c, g][0][:].bitcast(FP8X4), rhs_scale=ws_mx[c, g][1][:],
                    start=(g == 0), stop=(g == S_PASSES - 1),
                )
            return shared_sum

        whole = [slice(0, NC)]
        halves = [slice(0, NC // 2), slice(NC // 2, NC)]

        def gate_and_residual(n, parts=whole):
            i, c = unit[n]
            partial[n] = work.tile([P, NC], F32, name="partial", bufs=5)
            for s in parts:
                nc.vector.scalar_tensor_tensor(
                    out=partial[n][:, s], in0=routed_sum[n][:, s], scalar=gate_col[:, i : i + 1],
                    in1=x_sb[i, c][:, s], op0=MULT, op1=ADD,
                )

        def add_shared(n, shared_sum, parts=whole):
            total[n] = work.tile([P, NC], F32, name="total", bufs=4)
            for s in parts:
                nc.vector.tensor_tensor(out=total[n][:, s], in0=shared_sum[:, s], in1=partial[n][:, s], op=ADD)

        def routed_unit(n):
            routed_matmuls(n)
            gate_and_residual(n)

        def shared_unit(n):
            add_shared(n, shared_matmuls(n))

        def scale_y(n, engine, parts=whole):
            y[n] = work.tile([P, NC], F32, name="y", bufs=9)
            for s in parts:
                engine.tensor_tensor(
                    out=y[n][:, s], in0=total[n][:, s], in1=smooth_all[:, cols(unit[n][1])][:, s], op=MULT
                )

        def store_y(n):
            i, c = unit[n]
            nc.sync.dma_start(out=out_0[block(i), cols(c)], in_=y[n][:])

        def round_y(n, parts=whole):
            y_sorted[n] = work.tile([P, 2, P, 2], BF16, name="y_sorted", bufs=UNITS - TAIL_FROM)
            for s in parts:
                nc.scalar.copy(
                    out=y_sorted[n][:, :, s.start // 4 : s.stop // 4, :],
                    in_=y[n][:, s].rearrange("m (p u e) -> m u p e", u=2, e=2),
                )

        def turn_y(n, count, copy):
            i, c = unit[n]
            bank = tr_psum.tile([P, 4, P], F32, name="tr_bank")
            for j in range(count):
                words = y_sorted[n + j][:].rearrange("m u p e -> m (u p e)").bitcast(F32)
                for u in range(2):
                    nc.tensor.transpose(bank[:, 2 * j + u, :], words[:, block(u)], ident[:])
            turned = work.tile([P, 2 * NC], BF16, name="y_turned", bufs=5, align_bytes=64)
            zip_bank(turned[:, : count * NC], bank, count, copy)
            tokens = block(i, count)
            turned_ready.append((y_words[:, c, tokens], y_scales[:, c, tokens], turned[:, : count * NC]))

        def store_words(n0, n1):
            for c in sorted(set(unit[n][1] for n in range(n0, n1))):
                tiles = [unit[n][0] for n in range(n0, n1) if unit[n][1] == c]
                tokens = block(tiles[0], len(tiles))
                nc.sync.dma_start(
                    out=out_1[c, :, tokens, :].rearrange("p m t -> p (m t)").bitcast(I32),
                    in_=y_words[:, c, tokens].bitcast(I32),
                )

        def store_scales(c0, c1, second_queue):
            for quad in range(4):
                queue = second_queue if quad % 2 else nc.sync
                queue.dma_start(
                    out=out_2[c0:c1, 4 * quad : 4 * quad + 4, :].rearrange("g r m -> r g m").bitcast(I32),
                    in_=y_scales[32 * quad : 32 * quad + 4, c0:c1, :].bitcast(I32),
                )

        turn_hr(0)
        quantize(turned_ready, 2)
        spread_vectors()
        routed_matmuls(0)
        turn_hr(1)
        gate_and_residual(0)
        quantize(turned_ready, 2)
        turn_hr(2)
        group_ws(QUARTERS // 2)
        quantize(turned_ready, 1)
        group_ws(QUARTERS // 2)
        quantize(turned_ready, 1)
        routed_unit(1)
        turn_hs(0)
        turn_hs(1)
        quantize(weights_ready, 1)
        group_ws(QUARTERS)
        quantize(turned_ready, 1)
        routed_matmuls(2)
        quantize(weights_ready, 1)
        quantize(turned_ready, 1)
        turn_hr(3)
        sort_h(hs_raw[3], S_PASSES, "hs", 3, 2)
        gate_and_residual(2)
        quantize(turned_ready, 1)
        shared_unit(0)
        quantize(turned_ready, 1)
        scale_y(0, nc.vector)
        shared_unit(1)

        turn_hs(2)
        turn_hr(4)
        quantize(turned_ready, 1)
        scale_y(1, nc.vector)
        sort_h(hr_raw[5], R_PASSES, "hr", 5, 1)
        sort_h(hs_raw[4], S_PASSES, "hs", 4, 2)
        quantize(turned_ready, 1)
        routed_unit(3)
        quantize(turned_ready, 1)
        group_ws(QUARTERS // 2)
        shared_unit(2)

        turn_hs(3)
        turn_hr(5)
        turn_hs(4)
        quantize(turned_ready, 1)
        scale_y(2, nc.vector)
        quantize(turned_ready, 1)
        routed_unit(4)
        quantize(turned_ready, 2)
        group_ws(QUARTERS // 2)
        shared_unit(3)

        turn_hs(5)
        quantize(weights_ready, 1)
        scale_y(3, nc.vector)
        routed_unit(5)
        quantize(turned_ready, 1)
        group_ws(QUARTERS)
        shared_unit(4)
        quantize(weights_ready, 1)
        for n in range(RUN):
            round_y(n)
        for n in range(3):
            store_y(n)

        last = UNITS - 1
        for n in range(TILES, last):
            routed_unit(n)
            if n - 2 not in y:
                scale_y(n - 2, nc.vector)
                quantize(turned_ready, RUN // 2)
                quantize(weights_ready, 1)
            shared_unit(n - 1)
            if n % 2 == 1:
                scale_y(n - 1, nc.gpsimd)
            if n - 3 not in y_sorted:
                round_y(n - 3)
            store_y(n - 3)
            if n % RUN == RUN - 1 and n - 3 <= TAIL_FROM:
                for m in range(n - 3 - RUN, n - 3, 2):
                    turn_y(m, 2, nc.scalar.copy)
            if n % RUN == 2 and RUN <= n - 6 <= TAIL_FROM:
                store_words(n - 6 - RUN, n - 6)
                if n - 6 >= TILES:
                    store_scales(0, 1, nc.sync)
            group_ws(QUARTERS // 2)

        shared_unit(last - 1)
        scale_y(last - 2, nc.vector)
        scale_y(last - 1, nc.gpsimd)
        for n in (last - 3, last - 2):
            round_y(n)
            store_y(n)
        routed_matmuls(last)
        shared_last = shared_matmuls(last)
        gate_and_residual(last, halves)
        add_shared(last, shared_last, halves)
        scale_y(last, nc.vector, halves)
        turn_y(TAIL_FROM, 2, nc.scalar.copy)
        round_y(last - 1)
        store_y(last - 1)
        round_y(last, halves)
        store_y(last)
        for n in range(TAIL_FROM + 2, last - 1, 2):
            turn_y(n, 2, nc.vector.tensor_copy if n < last - 3 else nc.scalar.copy)
            quantize(turned_ready, 1)
            store_words(n - 2, n)
        quantize(turned_ready, 1)
        store_words(last - 3, last - 1)
        turn_y(last - 1, 1, nc.scalar.copy)
        turn_y(last, 1, nc.scalar.copy)
        quantize(turned_ready, 2)
        store_words(last - 1, UNITS)
        store_scales(1, CHUNKS, nc.scalar)
